import numpy as np
import ml_dtypes


def mxq(x, axis, fmt="e4m3"):
    dtype, down = {"e4m3": (ml_dtypes.float8_e4m3fn, 7), "e5m2": (ml_dtypes.float8_e5m2, 14)}[fmt]
    v = np.moveaxis(np.asarray(x, np.float32).astype(ml_dtypes.bfloat16).astype(np.float64), axis, -1)
    blocks = v.reshape(v.shape[:-1] + (-1, 32))
    amax = np.abs(blocks).max(-1, keepdims=True)
    byte = np.maximum(np.where(amax > 0, np.frexp(amax)[1] - 1 + 127, 0) - down, 1)
    scale = np.exp2(byte - 127.0)
    codes = (blocks / scale).astype(np.float32).astype(dtype).astype(np.float64)
    return np.moveaxis((codes * scale).reshape(v.shape), -1, axis)


WIDE = False


def mx_kscale(k):
    if not WIDE:
        return np.ones(k)
    levels = np.array([10, -10, 5, -5, 0])
    if k % 512:
        return np.exp2(np.random.permutation(np.resize(levels, k // 32))).repeat(32)
    a = np.empty((k // 512, 16))
    for p in range(k // 512):
        a[p, :8] = np.random.permutation(np.resize(levels, 8))
        for g in range(8):
            far = levels[np.abs(levels - a[p, g]) >= 10]
            a[p, g + 8] = far[np.random.randint(len(far))]
    return np.exp2(a.ravel()).repeat(32)


def f64(x):
    return np.asarray(x).astype(np.float64)


def striped(idx):
    return np.tile(idx.reshape(-1, 16).T, (8, 1)).astype(np.uint16)


def unstriped(offs):
    return offs[:16].T.reshape(-1).astype(np.int64)


E2M1 = np.array([0.0, 0.5, 1.0, 1.5, 2.0, 3.0, 4.0, 6.0, -0.0, -0.5, -1.0, -1.5, -2.0, -3.0, -4.0, -6.0])


def pack_weight(w, fmt):
    k, n = w.shape
    w = f64(np.asarray(w, np.float32).astype(ml_dtypes.bfloat16)).reshape(k // 32, 32, n)
    amax = np.abs(w).max(1)
    if fmt == "e4m3":
        byte = np.frexp(amax)[1] - 1 + 127 - 7
    else:
        mant, ex = np.frexp(amax / 6.0)
        byte = np.where(mant > 0.5, ex, ex - 1) + 127
    byte = np.clip(np.where(amax > 0, byte, 1), 1, 254)
    scaled = (w * np.exp2(127.0 - byte)[:, None, :]).reshape(k, n).astype(np.float32)
    by_word = np.ascontiguousarray(scaled.reshape(k // 512, 128, 4, n).transpose(0, 1, 3, 2))
    if fmt == "e4m3":
        words = by_word.astype(ml_dtypes.float8_e4m3fn).view(np.uint8)
    else:
        c = by_word.astype(ml_dtypes.float4_e2m1fn).view(np.uint8) & 0xF
        words = (c[..., 0::2] | (c[..., 1::2] << 4)).reshape(k // 512, 128, 2 * n)
    return np.ascontiguousarray(words), np.ascontiguousarray(byte.astype(np.uint8).reshape(k // 512, 16, n))


def unpack_weight(words, scales, fmt):
    g, _, n = scales.shape
    words = np.ascontiguousarray(words).reshape(g, 128, n, -1)
    if fmt == "e4m3":
        vals = words.view(ml_dtypes.float8_e4m3fn).astype(np.float64)
    else:
        nib = np.empty((g, 128, n, 4), np.uint8)
        nib[..., 0::2] = words & 0xF
        nib[..., 1::2] = words >> 4
        vals = E2M1[nib]
    vals = vals * np.repeat(np.exp2(scales.astype(np.float64) - 127.0), 8, axis=1)[..., None]
    return vals.transpose(0, 1, 3, 2).reshape(g * 512, n)


def gelu(v):
    return 0.5 * v * (1.0 + np.tanh(np.sqrt(2.0 / np.pi) * (v + 0.044715 * v**3)))


def striped8(idx):
    return np.concatenate([v.reshape(-1, 16).T for v in idx]).astype(np.uint16)


def unstriped8(offs):
    return np.stack([offs[16 * g:16 * g + 16].T.reshape(-1) for g in range(8)]).astype(np.int64)


def runs(v, idx8):
    k = np.arange(v.shape[0])
    return v[k[:, None], idx8[k % 512 // 64]]


K, M, H, N, T, S, T2 = 1024, 512, 1024, 512, 2048, 1024, 2048

def setup_inputs():
    n = np.random.standard_normal
    s1 = mx_kscale(K)[:, None]
    s2 = mx_kscale(M)[:, None]
    u = mx_kscale(H)[:, None]
    tab_words, tab_scales = pack_weight(n((K, T)) * s1, "e4m3")
    tab2_words, tab2_scales = pack_weight(n((M, T)) * s2, "e4m3")
    w4_words, w4_scales = pack_weight(0.28 * n((M, H)) / np.sqrt(M) / s2, "e2m1")
    return {
        "tab_words": tab_words, "tab_scales": tab_scales,
        "tab2_words": tab2_words, "tab2_scales": tab2_scales,
        "offs": striped8(np.stack([np.random.permutation(T)[:S] for _ in range(8)])),
        "offs2": striped(np.random.permutation(T)[:S]),
        "offs3": striped(np.random.permutation(T2)[:S]),
        "w1": (0.42 * n((K, H)) / np.sqrt(K) / s1).astype(np.float32),
        "w4_words": w4_words, "w4_scales": w4_scales,
        "dist": np.random.uniform(-1.5, 1.5, (H, S)).astype(np.float32),
        "gain": (np.exp(0.3 * n(H)) * u[:, 0]).astype(np.float32),
        "w2": (1.5 * n((H, N)) / np.sqrt(H) / u).astype(np.float32),
        "page1": n((N, T2)).astype(np.float32),
        "wgo": np.exp(0.3 * n((128, S))).astype(np.float32),
    }

def reference(tab_words, tab_scales, tab2_words, tab2_scales, offs, offs2, offs3, w1, w4_words, w4_scales, dist, gain, w2, page1, wgo):
    v = runs(unpack_weight(tab_words, tab_scales, "e4m3"), unstriped8(offs))
    v2 = unpack_weight(tab2_words, tab2_scales, "e4m3")[:, unstriped(offs2)]
    w4 = unpack_weight(w4_words, w4_scales, "e2m1")
    d = f64(dist)
    panel = (mxq(f64(w1), 0, "e4m3").T @ v) * d
    lens = (w4.T @ v2) + d
    z = np.sin(np.maximum(panel, lens)) * f64(gain)[:, None]
    y = mxq(f64(w2), 0, "e4m3").T @ mxq(z, 0, "e4m3")
    out = f64(page1).copy()
    out[:, unstriped(offs3)] = np.tile(f64(wgo), (N // 128, 1)) * y
    return out

@@ -1,0 +1,252 @@
+import math
+from contextlib import ExitStack
+
+import concourse.mybir as mybir
+
+K, M, H, N, T, S, T2 = 1024, 512, 1024, 512, 2048, 1024, 2048
+FLOPS = 2 * (K * H * S + M * H * S + H * N * S)
+
+F32 = mybir.dt.float32
+BF16 = mybir.dt.bfloat16
+I32 = mybir.dt.int32
+U32 = mybir.dt.uint32
+U16 = mybir.dt.uint16
+U8 = mybir.dt.uint8
+FP8X4 = mybir.dt.float8_e4m3fn_x4
+FP4X4 = mybir.dt.float4_e2m1fn_x4
+ALU = mybir.AluOpType
+ACT = mybir.ActivationFunctionType
+
+P = 128
+PACK = 4
+PASS = P * PACK
+CH = 512
+LC = CH // 16
+ROUND = 1.5 * 2.0**23
+
+
+def tile_list_moire_risk_meter_kernel(tc, tab_words, tab_scales, tab2_words, tab2_scales, offs, offs2, offs3,
+                                                w1, w4_words, w4_scales, dist, gain, w2, page1, wgo, out):
+    nc = tc.nc
+    with ExitStack() as ctx:
+        keep = ctx.enter_context(tc.tile_pool(name="keep", bufs=1))
+        work = ctx.enter_context(tc.tile_pool(name="work", bufs=2))
+        psum = ctx.enter_context(tc.psum_pool(name="psum", bufs=3))
+
+        def kt(name, shape, dtype):
+            return keep.tile(shape, dtype, name=name, align_bytes=64)
+
+        list1 = kt("list1", [P, S // 16], U16)
+        list2 = kt("list2", [P, S // 16], U16)
+        list3 = kt("list3", [P, S // 16], U16)
+        ts_win = kt("ts_win", [P, T], U8)
+        t2s_win = kt("t2s_win", [P, T], U8)
+        w4s_raw = kt("w4s_raw", [P, H], U8)
+        nc.vector.memset(ts_win[:].bitcast(I32), 0)
+        nc.gpsimd.memset(t2s_win[:].bitcast(I32), 0)
+        nc.gpsimd.memset(w4s_raw[:].bitcast(I32), 0)
+
+        nc.sync.dma_start(list1[:], offs)
+        tabw = [kt("tabw%d" % a, [P, T], I32) for a in range(2)]
+        tab2w = kt("tab2w", [P, T], I32)
+        w4_raw = kt("w4_raw", [P, 2 * H], U8)
+        gains = kt("gains", [P, 2, PACK], F32)
+        wgo_sb = kt("wgo_sb", [P, S], F32)
+        pages = [kt("page%d" % n, [P, T2], F32) for n in range(N // P)]
+
+        def load_words(dst, src):
+            nc.sync.dma_start(dst[:], src.rearrange("p t i -> p (t i)").bitcast(I32))
+
+        def load_rows(tag, src, bufs):
+            raw = work.tile([P, PACK, CH], F32, name=tag, tag=tag, bufs=bufs, align_bytes=64)
+            nc.sync.dma_start(raw[:], src.rearrange("(p i) c -> p i c", i=PACK))
+            return raw
+
+        def load_w1(a, b):
+            return load_rows("wraw", w1[a * PASS:(a + 1) * PASS, b * PASS:(b + 1) * PASS], 3)
+
+        def load_dist(c, b):
+            return load_rows("dist", dist[b * PASS:(b + 1) * PASS, c * CH:(c + 1) * CH], 3)
+
+        for a in range(2):
+            for e in range(2):
+                nc.scalar.dma_start(ts_win[4 * a + e:P:16, :].bitcast(I32), tab_scales[a, e:16:2, :].bitcast(I32))
+        load_words(tabw[0], tab_words[0])
+        nc.sync.dma_start(list2[:], offs2)
+        w1raw = {(0, 0): load_w1(0, 0)}
+        for q in range(4):
+            nc.scalar.dma_start(t2s_win[32 * q:32 * q + 4, :].bitcast(I32), tab2_scales[0, 4 * q:4 * q + 4, :].bitcast(I32))
+        load_words(tabw[1], tab_words[1])
+        w1raw[1, 0] = load_w1(1, 0)
+        for q in range(4):
+            nc.scalar.dma_start(w4s_raw[32 * q:32 * q + 4, :].bitcast(I32), w4_scales[0, 4 * q:4 * q + 4, :].bitcast(I32))
+        nc.sync.dma_start(w4_raw[:].bitcast(I32), w4_words[0].bitcast(I32))
+        load_words(tab2w, tab2_words[0])
+        dist_sb = {(0, 0): load_dist(0, 0)}
+        nc.scalar.dma_start(gains[:], gain.rearrange("(b p t) -> p b t", b=2, t=PACK))
+        w1raw[0, 1] = load_w1(0, 1)
+
+        ts_g = kt("ts_g", [P, S], U8)
+        v_scales = kt("v_scales", [P, S], U8)
+        nc.vector.tensor_copy(ts_g[:], ts_win[:].indirect(list1[:]))
+        nc.vector.tensor_copy(v_scales[:].bitcast(I32), ts_g[:].bitcast(I32))
+        for a in range(2):
+            for e in range(2):
+                nc.gpsimd.dma_start(v_scales[4 * a + 2 + e:P:32, :].bitcast(I32), ts_g[16 + 4 * a + e:P:32, :].bitcast(I32))
+        v2_scales = kt("v2_scales", [P, S], U8)
+        nc.vector.tensor_copy(v2_scales[:], t2s_win[:].indirect(list2[:]))
+
+        w4_p = kt("w4_p", [P, 2, 2 * PASS], U8)
+        w4s_p = kt("w4s_p", [P, 2, PASS], U8)
+        for b in range(2):
+            nc.gpsimd.tensor_copy(
+                w4_p[:, b, :].rearrange("p (t q y) -> p t q y", t=PACK, y=2),
+                w4_raw[:, 2 * PASS * b:2 * PASS * (b + 1)].rearrange("p (q t y) -> p t q y", t=PACK, y=2))
+            nc.gpsimd.tensor_copy(
+                w4s_p[:, b, :].rearrange("p (t q) -> p t q", t=PACK),
+                w4s_raw[:, PASS * b:PASS * (b + 1)].rearrange("p (q t) -> p t q", t=PACK))
+
+        v_words = {}
+        v2_words = {}
+
+        def gather_words(c):
+            for a in range(2):
+                v_words[a, c] = kt("vw%d%d" % (a, c), [P, CH], U32)
+                nc.vector.tensor_copy(v_words[a, c][:], tabw[a][:].bitcast(U32).indirect(list1[:, c * LC:(c + 1) * LC]))
+            v2_words[c] = kt("v2w%d" % c, [P, CH], U32)
+            nc.vector.tensor_copy(v2_words[c][:], tab2w[:].bitcast(U32).indirect(list2[:, c * LC:(c + 1) * LC]))
+
+        def quantize(name, grouped):
+            codes = kt(name + "c", [P, CH], U32)
+            scales = kt(name + "s", [P, CH], U8)
+            nc.vector.quantize_mx(out=codes[:].bitcast(FP8X4), scales=scales[:], in_=grouped[:])
+            return codes, scales
+
+        w1q = {}
+        w2q = {}
+        zq = {}
+
+        def prep_w1(a, b):
+            grouped = work.tile([P, PACK * CH], BF16, name="wbf", tag="wbf", align_bytes=64)
+            nc.scalar.copy(grouped[:].rearrange("p (t m i) -> p m i t", t=PACK, i=PACK),
+                           w1raw[a, b][:].rearrange("p i (m t) -> p m i t", t=PACK))
+            w1q[a, b] = quantize("w1q%d%d" % (a, b), grouped)
+
+        def prep_w2(b, raw):
+            grouped = work.tile([P, PACK * CH], BF16, name="wbf", tag="wbf", align_bytes=64)
+            nc.scalar.copy(grouped[:].rearrange("p (m e i) -> p m i e", e=4, i=PACK),
+                           raw[:].rearrange("p i (m e) -> p m i e", e=4))
+            w2q[b] = quantize("w2q%d" % b, grouped)
+
+        phase = {}
+        zrows = {}
+
+        def products(c, b, h):
+            cols = slice(c * CH, (c + 1) * CH)
+            u = work.tile([P, 2, CH], F32, name="u", tag="u", bufs=4)
+            lens = work.tile([P, 2, CH], F32, name="lens", tag="lens")
+            for s in range(2):
+                t = 2 * h + s
+                p1 = psum.tile([P, CH], F32, name="p1", tag="p1")
+                p2 = psum.tile([P, CH], F32, name="p2", tag="p2")
+                for a in range(2):
+                    codes, scales = w1q[a, b]
+                    nc.tensor.matmul_mx(out=p1[:], lhsT=codes[:, t * P:(t + 1) * P].bitcast(FP8X4),
+                                        lhsT_scale=scales[:, t * P:(t + 1) * P],
+                                        rhs=v_words[a, c][:].bitcast(FP8X4), rhs_scale=v_scales[4 * a:P, cols],
+                                        start=(a == 0), stop=(a == 1))
+                nc.tensor.matmul_mx(out=p2[:], lhsT=w4_p[:, b, 2 * P * t:2 * P * (t + 1)].bitcast(FP4X4),
+                                    lhsT_scale=w4s_p[:, b, t * P:(t + 1) * P],
+                                    rhs=v2_words[c][:].bitcast(FP8X4), rhs_scale=v2_scales[:, cols],
+                                    start=True, stop=True)
+                d = dist_sb[c, b][:, t, :]
+                nc.vector.scalar_tensor_tensor(u[:, s, :], p1[:], 1.0 / (2.0 * math.pi), d, ALU.mult, ALU.mult)
+                nc.vector.tensor_tensor(lens[:, s, :], p2[:], d, ALU.add)
+            nc.vector.scalar_tensor_tensor(u[:], lens[:], 1.0 / (2.0 * math.pi), u[:], ALU.mult, ALU.max)
+            turns = work.tile([P, 2, CH], U32, name="turns", tag="turns")
+            nc.scalar.activation(turns[:], u[:], ACT.Copy, bias=ROUND)
+            phase[c, b, h] = (u, turns)
+
+        def beats(c, b, h):
+            u, turns = phase[c, b, h]
+            nc.vector.scalar_tensor_tensor(u[:], turns[:].bitcast(I32), ROUND, u[:], ALU.subtract, ALU.subtract)
+            nc.scalar.activation(u[:], u[:], ACT.Sin, scale=-2.0 * math.pi)
+            if h == 0:
+                zrows[c, b] = work.tile([P, PACK, CH], BF16, name="zrows", tag="zrows")
+            for s in range(2):
+                t = 2 * h + s
+                nc.scalar.activation(zrows[c, b][:, t, :], u[:, s, :], ACT.Copy, scale=gains[:, b, t:t + 1])
+
+        def quantize_z(c, b):
+            grouped = work.tile([P, PACK * CH], BF16, name="zbf", tag="zbf", align_bytes=64)
+            nc.scalar.copy(grouped[:].rearrange("p (m e t) -> p m t e", e=4, t=PACK),
+                           zrows[c, b][:].rearrange("p t (m e) -> p m t e", e=4))
+            codes = work.tile([P, CH], U32, name="zc", tag="zc", bufs=3, align_bytes=64)
+            scales = work.tile([P, CH], U8, name="zs", tag="zs", bufs=3, align_bytes=64)
+            nc.vector.quantize_mx(out=codes[:].bitcast(FP8X4), scales=scales[:], in_=grouped[:])
+            zq[c, b] = (codes, scales)
+
+        scores = {}
+
+        def second(c):
+            for n in range(N // P):
+                y = psum.tile([P, CH], F32, name="y", tag="y", bufs=2)
+                for b in range(2):
+                    nc.tensor.matmul_mx(out=y[:], lhsT=w2q[b][0][:, n * P:(n + 1) * P].bitcast(FP8X4),
+                                        lhsT_scale=w2q[b][1][:, n * P:(n + 1) * P],
+                                        rhs=zq[c, b][0][:].bitcast(FP8X4), rhs_scale=zq[c, b][1][:],
+                                        start=(b == 0), stop=(b == 1))
+                scores[c, n] = work.tile([P, CH], F32, name="score", tag="score", bufs=6)
+                nc.scalar.copy(scores[c, n][:], y[:])
+
+        def place(c, n):
+            nc.vector.tensor_tensor(pages[n][:].indirect(list3[:, c * LC:(c + 1) * LC]), scores[c, n][:],
+                                    wgo_sb[:, c * CH:(c + 1) * CH], ALU.mult)
+
+        gather_words(0)
+        prep_w1(0, 0)
+        prep_w1(1, 0)
+        w1raw[1, 1] = load_w1(1, 1)
+        dist_sb[0, 1] = load_dist(0, 1)
+        gather_words(1)
+        prep_w1(0, 1)
+        w2raw = [load_rows("wraw", w2[0:PASS, :], 3)]
+        products(0, 0, 0)
+        prep_w1(1, 1)
+        w2raw.append(load_rows("wraw", w2[PASS:2 * PASS, :], 3))
+        dist_sb[1, 0] = load_dist(1, 0)
+        nc.sync.dma_start(list3[:], offs3)
+        nc.sync.dma_start(wgo_sb[:], wgo)
+        for n in range(N // P):
+            nc.sync.dma_start(pages[n][:], page1[n * P:(n + 1) * P, :])
+        products(0, 0, 1)
+        beats(0, 0, 0)
+        products(0, 1, 0)
+        dist_sb[1, 1] = load_dist(1, 1)
+        beats(0, 0, 1)
+        prep_w2(0, w2raw[0])
+        products(0, 1, 1)
+        beats(0, 1, 0)
+        quantize_z(0, 0)
+        products(1, 0, 0)
+        beats(0, 1, 1)
+        prep_w2(1, w2raw[1])
+        products(1, 0, 1)
+        beats(1, 0, 0)
+        quantize_z(0, 1)
+        second(0)
+        products(1, 1, 0)
+        beats(1, 0, 1)
+        place(0, 0)
+        products(1, 1, 1)
+        beats(1, 1, 0)
+        quantize_z(1, 0)
+        place(0, 1)
+        beats(1, 1, 1)
+        place(0, 2)
+        quantize_z(1, 1)
+        place(0, 3)
+        second(1)
+        for n in range(N // P):
+            place(1, n)
+            nc.sync.dma_start(out[n * P:(n + 1) * P, :], pages[n][:])

@@ -33,58 +33,56 @@ def tile_list_moire_risk_meter_kernel(tc, tab_words, tab_scales, tab2_words, tab
         work = ctx.enter_context(tc.tile_pool(name="work", bufs=2))
         psum = ctx.enter_context(tc.psum_pool(name="psum", bufs=3))
 
-        def kt(name, shape, dtype):
-            return keep.tile(shape, dtype, name=name, align_bytes=64)
+        def kt(name, shape, dtype, slot=None):
+            return keep.tile(shape, dtype, name=name, tag=slot or name, align_bytes=64)
 
         list1 = kt("list1", [P, S // 16], U16)
         list2 = kt("list2", [P, S // 16], U16)
         list3 = kt("list3", [P, S // 16], U16)
-        ts_win = kt("ts_win", [P, T], U8)
-        t2s_win = kt("t2s_win", [P, T], U8)
-        w4s_raw = kt("w4s_raw", [P, H], U8)
-        nc.vector.memset(ts_win[:].bitcast(I32), 0)
-        nc.gpsimd.memset(t2s_win[:].bitcast(I32), 0)
-        nc.gpsimd.memset(w4s_raw[:].bitcast(I32), 0)
-
-        nc.sync.dma_start(list1[:], offs)
-        tabw = [kt("tabw%d" % a, [P, T], I32) for a in range(2)]
-        tab2w = kt("tab2w", [P, T], I32)
-        w4_raw = kt("w4_raw", [P, 2 * H], U8)
+        ts_win = kt("ts_win", [P, T], U8, "slot_s")
+        t2s_win = kt("t2s_win", [P, T], U8, "slot_t")
+        nc.gpsimd.memset(ts_win[:].bitcast(I32), 0)
+        nc.vector.memset(t2s_win[:].bitcast(I32), 0)
+        w4_raw = kt("w4_raw", [P, 2 * H], U8, "slot_w4")
         gains = kt("gains", [P, 2, PACK], F32)
-        wgo_sb = kt("wgo_sb", [P, S], F32)
-        pages = [kt("page%d" % n, [P, T2], F32) for n in range(N // P)]
 
-        def load_words(dst, src):
-            nc.sync.dma_start(dst[:], src.rearrange("p t i -> p (t i)").bitcast(I32))
+        def load_words(name, src):
+            words = kt(name, [P, T], I32)
+            nc.sync.dma_start(words[:], src.rearrange("p t i -> p (t i)").bitcast(I32))
+            return words
 
-        def load_rows(tag, src, bufs):
-            raw = work.tile([P, PACK, CH], F32, name=tag, tag=tag, bufs=bufs, align_bytes=64)
+        def load_rows(slot, src):
+            raw = kt("raw", [P, PACK, CH], F32, slot)
             nc.sync.dma_start(raw[:], src.rearrange("(p i) c -> p i c", i=PACK))
             return raw
 
         def load_w1(a, b):
-            return load_rows("wraw", w1[a * PASS:(a + 1) * PASS, b * PASS:(b + 1) * PASS], 3)
+            return load_rows("slot_w%d" % a, w1[a * PASS:(a + 1) * PASS, b * PASS:(b + 1) * PASS])
 
-        def load_dist(c, b):
-            return load_rows("dist", dist[b * PASS:(b + 1) * PASS, c * CH:(c + 1) * CH], 3)
+        def load_dist(c, b, slot):
+            return load_rows(slot, dist[b * PASS:(b + 1) * PASS, c * CH:(c + 1) * CH])
 
+        def load_page(n, slot):
+            page = kt("page", [P, T2], F32, slot)
+            nc.sync.dma_start(page[:], page1[n * P:(n + 1) * P, :])
+            return page
+
+        nc.sync.dma_start(list1[:], offs)
+        nc.sync.dma_start(list2[:], offs2)
+        nc.sync.dma_start(list3[:], offs3)
+        nc.sync.dma_start(gains[:], gain.rearrange("(b p t) -> p b t", b=2, t=PACK))
+        nc.sync.dma_start(w4_raw[:].bitcast(I32), w4_words[0].bitcast(I32))
+        tabw = [load_words("tabw0", tab_words[0])]
+        w1raw = {(0, 0): load_w1(0, 0)}
         for a in range(2):
             for e in range(2):
-                nc.scalar.dma_start(ts_win[4 * a + e:P:16, :].bitcast(I32), tab_scales[a, e:16:2, :].bitcast(I32))
-        load_words(tabw[0], tab_words[0])
-        nc.sync.dma_start(list2[:], offs2)
-        w1raw = {(0, 0): load_w1(0, 0)}
-        for q in range(4):
-            nc.scalar.dma_start(t2s_win[32 * q:32 * q + 4, :].bitcast(I32), tab2_scales[0, 4 * q:4 * q + 4, :].bitcast(I32))
-        load_words(tabw[1], tab_words[1])
+                nc.sync.dma_start(ts_win[4 * a + e:P:16, :].bitcast(I32), tab_scales[a, e:16:2, :].bitcast(I32))
+        for q in range(2):
+            nc.sync.dma_start(t2s_win[32 * q:32 * q + 4, :].bitcast(I32), tab2_scales[0, 4 * q:4 * q + 4, :].bitcast(I32))
         w1raw[1, 0] = load_w1(1, 0)
-        for q in range(4):
-            nc.scalar.dma_start(w4s_raw[32 * q:32 * q + 4, :].bitcast(I32), w4_scales[0, 4 * q:4 * q + 4, :].bitcast(I32))
-        nc.sync.dma_start(w4_raw[:].bitcast(I32), w4_words[0].bitcast(I32))
-        load_words(tab2w, tab2_words[0])
-        dist_sb = {(0, 0): load_dist(0, 0)}
-        nc.scalar.dma_start(gains[:], gain.rearrange("(b p t) -> p b t", b=2, t=PACK))
-        w1raw[0, 1] = load_w1(0, 1)
+        tabw.append(load_words("tabw1", tab_words[1]))
+        for q in range(2, 4):
+            nc.sync.dma_start(t2s_win[32 * q:32 * q + 4, :].bitcast(I32), tab2_scales[0, 4 * q:4 * q + 4, :].bitcast(I32))
 
         ts_g = kt("ts_g", [P, S], U8)
         v_scales = kt("v_scales", [P, S], U8)
@@ -92,29 +90,39 @@ def tile_list_moire_risk_meter_kernel(tc, tab_words, tab_scales, tab2_words, tab
         nc.vector.tensor_copy(v_scales[:].bitcast(I32), ts_g[:].bitcast(I32))
         for a in range(2):
             for e in range(2):
-                nc.gpsimd.dma_start(v_scales[4 * a + 2 + e:P:32, :].bitcast(I32), ts_g[16 + 4 * a + e:P:32, :].bitcast(I32))
+                nc.sync.dma_start(v_scales[4 * a + 2 + e:P:32, :].bitcast(I32), ts_g[16 + 4 * a + e:P:32, :].bitcast(I32))
         v2_scales = kt("v2_scales", [P, S], U8)
         nc.vector.tensor_copy(v2_scales[:], t2s_win[:].indirect(list2[:]))
-
-        w4_p = kt("w4_p", [P, 2, 2 * PASS], U8)
-        w4s_p = kt("w4s_p", [P, 2, PASS], U8)
-        for b in range(2):
-            nc.gpsimd.tensor_copy(
-                w4_p[:, b, :].rearrange("p (t q y) -> p t q y", t=PACK, y=2),
-                w4_raw[:, 2 * PASS * b:2 * PASS * (b + 1)].rearrange("p (q t y) -> p t q y", t=PACK, y=2))
-            nc.gpsimd.tensor_copy(
-                w4s_p[:, b, :].rearrange("p (t q) -> p t q", t=PACK),
-                w4s_raw[:, PASS * b:PASS * (b + 1)].rearrange("p (q t) -> p t q", t=PACK))
 
         v_words = {}
         v2_words = {}
 
-        def gather_words(c):
-            for a in range(2):
-                v_words[a, c] = kt("vw%d%d" % (a, c), [P, CH], U32)
-                nc.vector.tensor_copy(v_words[a, c][:], tabw[a][:].bitcast(U32).indirect(list1[:, c * LC:(c + 1) * LC]))
+        def gather_tab(a, c):
+            v_words[a, c] = kt("vw%d%d" % (a, c), [P, CH], U32)
+            nc.vector.tensor_copy(v_words[a, c][:], tabw[a][:].bitcast(U32).indirect(list1[:, c * LC:(c + 1) * LC]))
+
+        def gather_tab2(c):
             v2_words[c] = kt("v2w%d" % c, [P, CH], U32)
             nc.vector.tensor_copy(v2_words[c][:], tab2w[:].bitcast(U32).indirect(list2[:, c * LC:(c + 1) * LC]))
+
+        gather_tab(0, 0)
+        gather_tab(0, 1)
+        dist_sb = {(0, 0): load_dist(0, 0, "tabw0")}
+        tab2w = load_words("tab2w", tab2_words[0])
+        w4s_raw = kt("w4s_raw", [P, H], U8, "slot_s")
+        nc.gpsimd.memset(w4s_raw[:].bitcast(I32), 0)
+        for q in range(4):
+            nc.sync.dma_start(w4s_raw[32 * q:32 * q + 4, :].bitcast(I32), w4_scales[0, 4 * q:4 * q + 4, :].bitcast(I32))
+
+        w4_p = kt("w4_p", [P, 2, 2 * PASS], U8)
+        w4s_p = kt("w4s_p", [P, 2, PASS], U8)
+        for b in range(2):
+            nc.vector.tensor_copy(
+                w4_p[:, b, :].bitcast(U16).rearrange("p (t q) -> p t q", t=PACK),
+                w4_raw[:, 2 * PASS * b:2 * PASS * (b + 1)].bitcast(U16).rearrange("p (q t) -> p t q", t=PACK))
+            nc.vector.tensor_copy(
+                w4s_p[:, b, :].rearrange("p (t q) -> p t q", t=PACK),
+                w4s_raw[:, PASS * b:PASS * (b + 1)].rearrange("p (q t) -> p t q", t=PACK))
 
         def quantize(name, grouped):
             codes = kt(name + "c", [P, CH], U32)
@@ -163,7 +171,7 @@ def tile_list_moire_risk_meter_kernel(tc, tab_words, tab_scales, tab2_words, tab
                 nc.vector.scalar_tensor_tensor(u[:, s, :], p1[:], 1.0 / (2.0 * math.pi), d, ALU.mult, ALU.mult)
                 nc.vector.tensor_tensor(lens[:, s, :], p2[:], d, ALU.add)
             nc.vector.scalar_tensor_tensor(u[:], lens[:], 1.0 / (2.0 * math.pi), u[:], ALU.mult, ALU.max)
-            turns = work.tile([P, 2, CH], U32, name="turns", tag="turns")
+            turns = work.tile([P, 2, CH], U32, name="turns", tag="turns%d" % h, bufs=1)
             nc.scalar.activation(turns[:], u[:], ACT.Copy, bias=ROUND)
             phase[c, b, h] = (u, turns)
 
@@ -172,7 +180,7 @@ def tile_list_moire_risk_meter_kernel(tc, tab_words, tab_scales, tab2_words, tab
             nc.vector.scalar_tensor_tensor(u[:], turns[:].bitcast(I32), ROUND, u[:], ALU.subtract, ALU.subtract)
             nc.scalar.activation(u[:], u[:], ACT.Sin, scale=-2.0 * math.pi)
             if h == 0:
-                zrows[c, b] = work.tile([P, PACK, CH], BF16, name="zrows", tag="zrows")
+                zrows[c, b] = work.tile([P, PACK, CH], BF16, name="zrows", tag="zrows%d" % b, bufs=1)
             for s in range(2):
                 t = 2 * h + s
                 nc.scalar.activation(zrows[c, b][:, t, :], u[:, s, :], ACT.Copy, scale=gains[:, b, t:t + 1])
@@ -181,72 +189,78 @@ def tile_list_moire_risk_meter_kernel(tc, tab_words, tab_scales, tab2_words, tab
             grouped = work.tile([P, PACK * CH], BF16, name="zbf", tag="zbf", align_bytes=64)
             nc.scalar.copy(grouped[:].rearrange("p (m e t) -> p m t e", e=4, t=PACK),
                            zrows[c, b][:].rearrange("p t (m e) -> p m t e", e=4))
-            codes = work.tile([P, CH], U32, name="zc", tag="zc", bufs=3, align_bytes=64)
-            scales = work.tile([P, CH], U8, name="zs", tag="zs", bufs=3, align_bytes=64)
+            codes = work.tile([P, CH], U32, name="zc", tag="zc", bufs=4, align_bytes=64)
+            scales = work.tile([P, CH], U8, name="zs", tag="zs", bufs=4, align_bytes=64)
             nc.vector.quantize_mx(out=codes[:].bitcast(FP8X4), scales=scales[:], in_=grouped[:])
             zq[c, b] = (codes, scales)
 
         scores = {}
 
-        def second(c):
-            for n in range(N // P):
+        def second(c, tiles, tag="score", bufs=4):
+            for n in tiles:
                 y = psum.tile([P, CH], F32, name="y", tag="y", bufs=2)
                 for b in range(2):
                     nc.tensor.matmul_mx(out=y[:], lhsT=w2q[b][0][:, n * P:(n + 1) * P].bitcast(FP8X4),
                                         lhsT_scale=w2q[b][1][:, n * P:(n + 1) * P],
                                         rhs=zq[c, b][0][:].bitcast(FP8X4), rhs_scale=zq[c, b][1][:],
                                         start=(b == 0), stop=(b == 1))
-                scores[c, n] = work.tile([P, CH], F32, name="score", tag="score", bufs=6)
+                scores[c, n] = work.tile([P, CH], F32, name="score", tag=tag, bufs=bufs)
                 nc.scalar.copy(scores[c, n][:], y[:])
 
         def place(c, n):
             nc.vector.tensor_tensor(pages[n][:].indirect(list3[:, c * LC:(c + 1) * LC]), scores[c, n][:],
                                     wgo_sb[:, c * CH:(c + 1) * CH], ALU.mult)
 
-        gather_words(0)
         prep_w1(0, 0)
+        gather_tab(1, 0)
         prep_w1(1, 0)
+        gather_tab2(0)
+        w1raw[0, 1] = load_w1(0, 1)
         w1raw[1, 1] = load_w1(1, 1)
-        dist_sb[0, 1] = load_dist(0, 1)
-        gather_words(1)
-        prep_w1(0, 1)
-        w2raw = [load_rows("wraw", w2[0:PASS, :], 3)]
+        dist_sb[0, 1] = load_dist(0, 1, "slot_t")
+        gather_tab(1, 1)
         products(0, 0, 0)
-        prep_w1(1, 1)
-        w2raw.append(load_rows("wraw", w2[PASS:2 * PASS, :], 3))
-        dist_sb[1, 0] = load_dist(1, 0)
-        nc.sync.dma_start(list3[:], offs3)
+        prep_w1(0, 1)
+        gather_tab2(1)
+        dist_sb[1, 0] = load_dist(1, 0, "tabw1")
+        wgo_sb = kt("wgo_sb", [P, S], F32, "slot_w4")
         nc.sync.dma_start(wgo_sb[:], wgo)
-        for n in range(N // P):
-            nc.sync.dma_start(pages[n][:], page1[n * P:(n + 1) * P, :])
+        pages = [load_page(0, "tab2w")]
         products(0, 0, 1)
+        prep_w1(1, 1)
+        w2raw = [load_rows("slot_w%d" % b, w2[b * PASS:(b + 1) * PASS, :]) for b in range(2)]
+        pages.append(load_page(1, "tabw0"))
         beats(0, 0, 0)
         products(0, 1, 0)
-        dist_sb[1, 1] = load_dist(1, 1)
         beats(0, 0, 1)
         prep_w2(0, w2raw[0])
         products(0, 1, 1)
+        dist_sb[1, 1] = load_dist(1, 1, "slot_t")
         beats(0, 1, 0)
         quantize_z(0, 0)
         products(1, 0, 0)
         beats(0, 1, 1)
         prep_w2(1, w2raw[1])
+        pages.extend(load_page(2 + b, "slot_w%d" % b) for b in range(2))
         products(1, 0, 1)
         beats(1, 0, 0)
         quantize_z(0, 1)
-        second(0)
+        second(0, [0])
         products(1, 1, 0)
         beats(1, 0, 1)
         place(0, 0)
         products(1, 1, 1)
         beats(1, 1, 0)
+        second(0, [1], "turns0", 1)
         quantize_z(1, 0)
-        place(0, 1)
         beats(1, 1, 1)
+        second(0, [2], "turns1", 1)
+        place(0, 1)
         place(0, 2)
         quantize_z(1, 1)
+        second(0, [3], "zrows1", 1)
         place(0, 3)
-        second(1)
+        second(1, range(N // P))
         for n in range(N // P):
             place(1, n)
             nc.sync.dma_start(out[n * P:(n + 1) * P, :], pages[n][:])

@@ -59,38 +59,45 @@ def tile_list_moire_risk_meter_kernel(tc, tab_words, tab_scales, tab2_words, tab
         def load_w1(a, b):
             return load_rows("slot_w%d" % a, w1[a * PASS:(a + 1) * PASS, b * PASS:(b + 1) * PASS])
 
-        def load_dist(c, b, slot):
-            return load_rows(slot, dist[b * PASS:(b + 1) * PASS, c * CH:(c + 1) * CH])
+        dist_sb = {}
+
+        def load_dist(c, b):
+            rows = dist[b * PASS:(b + 1) * PASS, c * CH:(c + 1) * CH].rearrange("(p t) j -> p t j", t=PACK)
+            for h in range(2):
+                dist_sb[c, b, h] = kt("dist", [P, 2, CH], F32, "dist%d%d" % (b, h))
+                nc.sync.dma_start(dist_sb[c, b, h][:], rows[:, 2 * h:2 * h + 2, :])
 
         def load_page(n, slot):
             page = kt("page", [P, T2], F32, slot)
             nc.sync.dma_start(page[:], page1[n * P:(n + 1) * P, :])
             return page
 
+        w4s_raw = kt("w4s_raw", [P, H], U8)
+        nc.gpsimd.memset(w4s_raw[:].bitcast(I32), 0)
+
+        def load_plane(plane, rows, q):
+            nc.sync.dma_start(plane[32 * q:32 * q + 4, :].bitcast(I32), rows[0, 4 * q:4 * q + 4, :].bitcast(I32))
+
         nc.sync.dma_start(list1[:], offs)
-        nc.sync.dma_start(list2[:], offs2)
-        nc.sync.dma_start(list3[:], offs3)
-        nc.sync.dma_start(gains[:], gain.rearrange("(b p t) -> p b t", b=2, t=PACK))
-        nc.sync.dma_start(w4_raw[:].bitcast(I32), w4_words[0].bitcast(I32))
         tabw = [load_words("tabw0", tab_words[0])]
         w1raw = {(0, 0): load_w1(0, 0)}
         for a in range(2):
             for e in range(2):
                 nc.sync.dma_start(ts_win[4 * a + e:P:16, :].bitcast(I32), tab_scales[a, e:16:2, :].bitcast(I32))
-        for q in range(2):
-            nc.sync.dma_start(t2s_win[32 * q:32 * q + 4, :].bitcast(I32), tab2_scales[0, 4 * q:4 * q + 4, :].bitcast(I32))
-        w1raw[1, 0] = load_w1(1, 0)
+        nc.sync.dma_start(list2[:], offs2)
+        load_plane(t2s_win, tab2_scales, 0)
         tabw.append(load_words("tabw1", tab_words[1]))
-        for q in range(2, 4):
-            nc.sync.dma_start(t2s_win[32 * q:32 * q + 4, :].bitcast(I32), tab2_scales[0, 4 * q:4 * q + 4, :].bitcast(I32))
+        w1raw[1, 0] = load_w1(1, 0)
+        for q in range(1, 4):
+            load_plane(t2s_win, tab2_scales, q)
+        nc.sync.dma_start(w4_raw[:].bitcast(I32), w4_words[0].bitcast(I32))
+        for q in range(2):
+            load_plane(w4s_raw, w4_scales, q)
 
         ts_g = kt("ts_g", [P, S], U8)
         v_scales = kt("v_scales", [P, S], U8)
         nc.vector.tensor_copy(ts_g[:], ts_win[:].indirect(list1[:]))
         nc.vector.tensor_copy(v_scales[:].bitcast(I32), ts_g[:].bitcast(I32))
-        for a in range(2):
-            for e in range(2):
-                nc.sync.dma_start(v_scales[4 * a + 2 + e:P:32, :].bitcast(I32), ts_g[16 + 4 * a + e:P:32, :].bitcast(I32))
         v2_scales = kt("v2_scales", [P, S], U8)
         nc.vector.tensor_copy(v2_scales[:], t2s_win[:].indirect(list2[:]))
 
@@ -107,12 +114,13 @@ def tile_list_moire_risk_meter_kernel(tc, tab_words, tab_scales, tab2_words, tab
 
         gather_tab(0, 0)
         gather_tab(0, 1)
-        dist_sb = {(0, 0): load_dist(0, 0, "tabw0")}
+        w1raw[0, 1] = load_rows("tabw0", w1[0:PASS, PASS:2 * PASS])
         tab2w = load_words("tab2w", tab2_words[0])
-        w4s_raw = kt("w4s_raw", [P, H], U8, "slot_s")
-        nc.gpsimd.memset(w4s_raw[:].bitcast(I32), 0)
-        for q in range(4):
-            nc.sync.dma_start(w4s_raw[32 * q:32 * q + 4, :].bitcast(I32), w4_scales[0, 4 * q:4 * q + 4, :].bitcast(I32))
+        for a in range(2):
+            for e in range(2):
+                nc.sync.dma_start(v_scales[4 * a + 2 + e:P:32, :].bitcast(I32), ts_g[16 + 4 * a + e:P:32, :].bitcast(I32))
+        for q in range(2, 4):
+            load_plane(w4s_raw, w4_scales, q)
 
         w4_p = kt("w4_p", [P, 2, 2 * PASS], U8)
         w4s_p = kt("w4s_p", [P, 2, PASS], U8)
@@ -151,8 +159,8 @@ def tile_list_moire_risk_meter_kernel(tc, tab_words, tab_scales, tab2_words, tab
 
         def products(c, b, h):
             cols = slice(c * CH, (c + 1) * CH)
-            u = work.tile([P, 2, CH], F32, name="u", tag="u", bufs=4)
-            lens = work.tile([P, 2, CH], F32, name="lens", tag="lens")
+            u = kt("u", [P, 2, CH], F32, "u%d" % ((4 * c + 2 * b + h) % 3))
+            lens = kt("lens", [P, 2, CH], F32, "lens%d" % ((4 * c + 2 * b + h) % 4))
             for s in range(2):
                 t = 2 * h + s
                 p1 = psum.tile([P, CH], F32, name="p1", tag="p1")
@@ -167,28 +175,45 @@ def tile_list_moire_risk_meter_kernel(tc, tab_words, tab_scales, tab2_words, tab
                                     lhsT_scale=w4s_p[:, b, t * P:(t + 1) * P],
                                     rhs=v2_words[c][:].bitcast(FP8X4), rhs_scale=v2_scales[:, cols],
                                     start=True, stop=True)
-                d = dist_sb[c, b][:, t, :]
+                d = dist_sb[c, b, h][:, s, :]
                 nc.vector.scalar_tensor_tensor(u[:, s, :], p1[:], 1.0 / (2.0 * math.pi), d, ALU.mult, ALU.mult)
                 nc.vector.tensor_tensor(lens[:, s, :], p2[:], d, ALU.add)
             nc.vector.scalar_tensor_tensor(u[:], lens[:], 1.0 / (2.0 * math.pi), u[:], ALU.mult, ALU.max)
-            turns = work.tile([P, 2, CH], U32, name="turns", tag="turns%d" % h, bufs=1)
+            turns = kt("turns", [P, 2, CH], U32, "turns%d" % ((4 * c + 2 * b + h) % 3))
             nc.scalar.activation(turns[:], u[:], ACT.Copy, bias=ROUND)
             phase[c, b, h] = (u, turns)
 
-        def beats(c, b, h):
+        rests = {}
+
+        def reduce_phase(c, b, h):
             u, turns = phase[c, b, h]
-            nc.vector.scalar_tensor_tensor(u[:], turns[:].bitcast(I32), ROUND, u[:], ALU.subtract, ALU.subtract)
-            nc.scalar.activation(u[:], u[:], ACT.Sin, scale=-2.0 * math.pi)
+            rest = kt("rest", [P, 2, CH], F32, "lens%d" % ((4 * c + 2 * b + h + (2 if c + b == 2 else 1)) % 4))
+            nc.vector.scalar_tensor_tensor(rest[:], turns[:].bitcast(I32), ROUND, u[:], ALU.subtract, ALU.subtract)
+            rests[c, b, h] = rest
+
+        def wave(c, b, h):
+            rest = rests[c, b, h]
+            nc.scalar.activation(rest[:], rest[:], ACT.Sin, scale=-2.0 * math.pi)
             if h == 0:
-                zrows[c, b] = work.tile([P, PACK, CH], BF16, name="zrows", tag="zrows%d" % b, bufs=1)
+                zrows[c, b] = kt("zrows", [P, PACK, CH], BF16, "zrows%d" % b)
             for s in range(2):
                 t = 2 * h + s
-                nc.scalar.activation(zrows[c, b][:, t, :], u[:, s, :], ACT.Copy, scale=gains[:, b, t:t + 1])
+                nc.scalar.activation(zrows[c, b][:, t, :], rest[:, s, :], ACT.Copy, scale=gains[:, b, t:t + 1])
 
-        def quantize_z(c, b):
+        zgrouped = {}
+
+        def beats(c, b, h):
+            reduce_phase(c, b, h)
+            wave(c, b, h)
+
+        def weave_z(c, b):
             grouped = work.tile([P, PACK * CH], BF16, name="zbf", tag="zbf", align_bytes=64)
             nc.scalar.copy(grouped[:].rearrange("p (m e t) -> p m t e", e=4, t=PACK),
                            zrows[c, b][:].rearrange("p t (m e) -> p m t e", e=4))
+            zgrouped[c, b] = grouped
+
+        def quantize_z(c, b):
+            grouped = zgrouped[c, b]
             codes = work.tile([P, CH], U32, name="zc", tag="zc", bufs=4, align_bytes=64)
             scales = work.tile([P, CH], U8, name="zs", tag="zs", bufs=4, align_bytes=64)
             nc.vector.quantize_mx(out=codes[:].bitcast(FP8X4), scales=scales[:], in_=grouped[:])
@@ -196,7 +221,7 @@ def tile_list_moire_risk_meter_kernel(tc, tab_words, tab_scales, tab2_words, tab
 
         scores = {}
 
-        def second(c, tiles, tag="score", bufs=4):
+        def second(c, tiles, tag=None):
             for n in tiles:
                 y = psum.tile([P, CH], F32, name="y", tag="y", bufs=2)
                 for b in range(2):
@@ -204,7 +229,7 @@ def tile_list_moire_risk_meter_kernel(tc, tab_words, tab_scales, tab2_words, tab
                                         lhsT_scale=w2q[b][1][:, n * P:(n + 1) * P],
                                         rhs=zq[c, b][0][:].bitcast(FP8X4), rhs_scale=zq[c, b][1][:],
                                         start=(b == 0), stop=(b == 1))
-                scores[c, n] = work.tile([P, CH], F32, name="score", tag=tag, bufs=bufs)
+                scores[c, n] = kt("score", [P, CH], F32, tag or "score%d" % n)
                 nc.scalar.copy(scores[c, n][:], y[:])
 
         def place(c, n):
@@ -214,51 +239,60 @@ def tile_list_moire_risk_meter_kernel(tc, tab_words, tab_scales, tab2_words, tab
         prep_w1(0, 0)
         gather_tab(1, 0)
         prep_w1(1, 0)
-        gather_tab2(0)
-        w1raw[0, 1] = load_w1(0, 1)
-        w1raw[1, 1] = load_w1(1, 1)
-        dist_sb[0, 1] = load_dist(0, 1, "slot_t")
-        gather_tab(1, 1)
-        products(0, 0, 0)
         prep_w1(0, 1)
-        gather_tab2(1)
-        dist_sb[1, 0] = load_dist(1, 0, "tabw1")
-        wgo_sb = kt("wgo_sb", [P, S], F32, "slot_w4")
-        nc.sync.dma_start(wgo_sb[:], wgo)
-        pages = [load_page(0, "tab2w")]
-        products(0, 0, 1)
+        gather_tab2(0)
+        w1raw[1, 1] = load_rows("slot_w0", w1[PASS:2 * PASS, PASS:2 * PASS])
+        load_dist(0, 0)
+        nc.sync.dma_start(gains[:], gain.rearrange("(b p t) -> p b t", b=2, t=PACK))
+        nc.sync.dma_start(list3[:], offs3)
+        gather_tab(1, 1)
         prep_w1(1, 1)
-        w2raw = [load_rows("slot_w%d" % b, w2[b * PASS:(b + 1) * PASS, :]) for b in range(2)]
-        pages.append(load_page(1, "tabw0"))
-        beats(0, 0, 0)
+        w2raw = [load_rows("slot_w1", w2[0:PASS, :])]
+        load_dist(0, 1)
+        w2raw.append(load_rows("tabw0", w2[PASS:2 * PASS, :]))
+        products(0, 0, 0)
+        gather_tab2(1)
+        products(0, 0, 1)
+        load_dist(1, 0)
         products(0, 1, 0)
-        beats(0, 0, 1)
-        prep_w2(0, w2raw[0])
+        beats(0, 0, 0)
         products(0, 1, 1)
-        dist_sb[1, 1] = load_dist(1, 1, "slot_t")
-        beats(0, 1, 0)
-        quantize_z(0, 0)
+        load_dist(1, 1)
+        wgo_sb = kt("wgo_sb", [P, S], F32, "tabw1")
+        nc.sync.dma_start(wgo_sb[:], wgo)
+        beats(0, 0, 1)
+        weave_z(0, 0)
+        prep_w2(0, w2raw[0])
         products(1, 0, 0)
-        beats(0, 1, 1)
+        beats(0, 1, 0)
         prep_w2(1, w2raw[1])
-        pages.extend(load_page(2 + b, "slot_w%d" % b) for b in range(2))
+        pages = [load_page(b, ("slot_w1", "tabw0")[b]) for b in range(2)]
         products(1, 0, 1)
-        beats(1, 0, 0)
-        quantize_z(0, 1)
-        second(0, [0])
+        pages.append(load_page(2, "tab2w"))
+        beats(0, 1, 1)
+        weave_z(0, 1)
+        quantize_z(0, 0)
         products(1, 1, 0)
+        beats(1, 0, 0)
         beats(1, 0, 1)
-        place(0, 0)
         products(1, 1, 1)
-        beats(1, 1, 0)
-        second(0, [1], "turns0", 1)
-        quantize_z(1, 0)
-        beats(1, 1, 1)
-        second(0, [2], "turns1", 1)
+        quantize_z(0, 1)
+        pages.append(load_page(3, "slot_w0"))
+        reduce_phase(1, 1, 0)
+        second(0, [0], "turns0")
+        reduce_phase(1, 1, 1)
+        second(0, [1], "turns1")
+        second(0, [2], "u1")
+        weave_z(1, 0)
+        wave(1, 1, 0)
+        wave(1, 1, 1)
+        weave_z(1, 1)
+        place(0, 0)
         place(0, 1)
+        quantize_z(1, 0)
         place(0, 2)
         quantize_z(1, 1)
-        second(0, [3], "zrows1", 1)
+        second(0, [3], "zrows1")
         place(0, 3)
         second(1, range(N // P))
         for n in range(N // P):

@@ -61,9 +61,9 @@ def tile_list_moire_risk_meter_kernel(tc, tab_words, tab_scales, tab2_words, tab
 
         dist_sb = {}
 
-        def load_dist(c, b):
+        def load_dist(c, b, halves=range(2)):
             rows = dist[b * PASS:(b + 1) * PASS, c * CH:(c + 1) * CH].rearrange("(p t) j -> p t j", t=PACK)
-            for h in range(2):
+            for h in halves:
                 dist_sb[c, b, h] = kt("dist", [P, 2, CH], F32, "dist%d%d" % (b, h))
                 nc.sync.dma_start(dist_sb[c, b, h][:], rows[:, 2 * h:2 * h + 2, :])
 
@@ -80,19 +80,18 @@ def tile_list_moire_risk_meter_kernel(tc, tab_words, tab_scales, tab2_words, tab
 
         nc.sync.dma_start(list1[:], offs)
         tabw = [load_words("tabw0", tab_words[0])]
-        w1raw = {(0, 0): load_w1(0, 0)}
+        nc.sync.dma_start(list2[:], offs2)
+        nc.sync.dma_start(w4_raw[:].bitcast(I32), w4_words[0].bitcast(I32))
         for a in range(2):
             for e in range(2):
                 nc.sync.dma_start(ts_win[4 * a + e:P:16, :].bitcast(I32), tab_scales[a, e:16:2, :].bitcast(I32))
-        nc.sync.dma_start(list2[:], offs2)
-        load_plane(t2s_win, tab2_scales, 0)
+        w1raw = {(0, 0): load_w1(0, 0)}
         tabw.append(load_words("tabw1", tab_words[1]))
-        w1raw[1, 0] = load_w1(1, 0)
-        for q in range(1, 4):
+        for q in range(4):
             load_plane(t2s_win, tab2_scales, q)
-        nc.sync.dma_start(w4_raw[:].bitcast(I32), w4_words[0].bitcast(I32))
         for q in range(2):
             load_plane(w4s_raw, w4_scales, q)
+        w1raw[1, 0] = load_w1(1, 0)
 
         ts_g = kt("ts_g", [P, S], U8)
         v_scales = kt("v_scales", [P, S], U8)
@@ -114,7 +113,6 @@ def tile_list_moire_risk_meter_kernel(tc, tab_words, tab_scales, tab2_words, tab
 
         gather_tab(0, 0)
         gather_tab(0, 1)
-        w1raw[0, 1] = load_rows("tabw0", w1[0:PASS, PASS:2 * PASS])
         tab2w = load_words("tab2w", tab2_words[0])
         for a in range(2):
             for e in range(2):
@@ -159,8 +157,8 @@ def tile_list_moire_risk_meter_kernel(tc, tab_words, tab_scales, tab2_words, tab
 
         def products(c, b, h):
             cols = slice(c * CH, (c + 1) * CH)
-            u = kt("u", [P, 2, CH], F32, "u%d" % ((4 * c + 2 * b + h) % 3))
-            lens = kt("lens", [P, 2, CH], F32, "lens%d" % ((4 * c + 2 * b + h) % 4))
+            u = kt("u", [P, 2, CH], F32, "u%d" % (2 * b + h))
+            lens = kt("lens", [P, 2, CH], F32, "lens%d" % h)
             for s in range(2):
                 t = 2 * h + s
                 p1 = psum.tile([P, CH], F32, name="p1", tag="p1")
@@ -179,16 +177,19 @@ def tile_list_moire_risk_meter_kernel(tc, tab_words, tab_scales, tab2_words, tab
                 nc.vector.scalar_tensor_tensor(u[:, s, :], p1[:], 1.0 / (2.0 * math.pi), d, ALU.mult, ALU.mult)
                 nc.vector.tensor_tensor(lens[:, s, :], p2[:], d, ALU.add)
             nc.vector.scalar_tensor_tensor(u[:], lens[:], 1.0 / (2.0 * math.pi), u[:], ALU.mult, ALU.max)
-            turns = kt("turns", [P, 2, CH], U32, "turns%d" % ((4 * c + 2 * b + h) % 3))
-            nc.scalar.activation(turns[:], u[:], ACT.Copy, bias=ROUND)
+            turns = kt("turns", [P, 2, CH], I32, "turns%d" % h)
+            if (c, b, h) == (1, 1, 1):
+                nc.scalar.activation(turns[:].bitcast(U32), u[:], ACT.Copy, bias=ROUND)
+            else:
+                nc.gpsimd.tensor_scalar(turns[:], u[:], 1.0, ROUND, ALU.mult, ALU.add)
             phase[c, b, h] = (u, turns)
 
         rests = {}
 
         def reduce_phase(c, b, h):
             u, turns = phase[c, b, h]
-            rest = kt("rest", [P, 2, CH], F32, "lens%d" % ((4 * c + 2 * b + h + (2 if c + b == 2 else 1)) % 4))
-            nc.vector.scalar_tensor_tensor(rest[:], turns[:].bitcast(I32), ROUND, u[:], ALU.subtract, ALU.subtract)
+            rest = u
+            nc.vector.scalar_tensor_tensor(rest[:], turns[:], ROUND, u[:], ALU.subtract, ALU.subtract)
             rests[c, b, h] = rest
 
         def wave(c, b, h):
@@ -239,52 +240,53 @@ def tile_list_moire_risk_meter_kernel(tc, tab_words, tab_scales, tab2_words, tab
         prep_w1(0, 0)
         gather_tab(1, 0)
         prep_w1(1, 0)
-        prep_w1(0, 1)
         gather_tab2(0)
-        w1raw[1, 1] = load_rows("slot_w0", w1[PASS:2 * PASS, PASS:2 * PASS])
-        load_dist(0, 0)
-        nc.sync.dma_start(gains[:], gain.rearrange("(b p t) -> p b t", b=2, t=PACK))
-        nc.sync.dma_start(list3[:], offs3)
+        load_dist(0, 0, [0])
+        w1raw[0, 1] = load_w1(0, 1)
+        load_dist(0, 0, [1])
+        w1raw[1, 1] = load_w1(1, 1)
+        prep_w1(0, 1)
         gather_tab(1, 1)
         prep_w1(1, 1)
-        w2raw = [load_rows("slot_w1", w2[0:PASS, :])]
         load_dist(0, 1)
-        w2raw.append(load_rows("tabw0", w2[PASS:2 * PASS, :]))
+        nc.sync.dma_start(gains[:], gain.rearrange("(b p t) -> p b t", b=2, t=PACK))
+        w2raw = [load_rows("tabw%d" % b, w2[b * PASS:(b + 1) * PASS, :]) for b in range(2)]
+        nc.sync.dma_start(list3[:], offs3)
         products(0, 0, 0)
         gather_tab2(1)
         products(0, 0, 1)
         load_dist(1, 0)
-        products(0, 1, 0)
         beats(0, 0, 0)
-        products(0, 1, 1)
-        load_dist(1, 1)
-        wgo_sb = kt("wgo_sb", [P, S], F32, "tabw1")
-        nc.sync.dma_start(wgo_sb[:], wgo)
+        products(0, 1, 0)
         beats(0, 0, 1)
         weave_z(0, 0)
         prep_w2(0, w2raw[0])
-        products(1, 0, 0)
+        products(0, 1, 1)
+        load_dist(1, 1)
+        wgo_sb = kt("wgo_sb", [P, S], F32, "slot_w0")
+        nc.sync.dma_start(wgo_sb[:], wgo)
         beats(0, 1, 0)
         prep_w2(1, w2raw[1])
-        pages = [load_page(b, ("slot_w1", "tabw0")[b]) for b in range(2)]
-        products(1, 0, 1)
+        pages = [load_page(b, "tabw%d" % b) for b in range(2)]
         pages.append(load_page(2, "tab2w"))
+        pages.append(load_page(3, "slot_w1"))
+        products(1, 0, 0)
         beats(0, 1, 1)
         weave_z(0, 1)
         quantize_z(0, 0)
-        products(1, 1, 0)
+        products(1, 0, 1)
         beats(1, 0, 0)
-        beats(1, 0, 1)
-        products(1, 1, 1)
+        products(1, 1, 0)
         quantize_z(0, 1)
-        pages.append(load_page(3, "slot_w0"))
+        beats(1, 0, 1)
+        second(0, [0], "u1")
+        weave_z(1, 0)
+        products(1, 1, 1)
         reduce_phase(1, 1, 0)
-        second(0, [0], "turns0")
         reduce_phase(1, 1, 1)
         second(0, [1], "turns1")
-        second(0, [2], "u1")
-        weave_z(1, 0)
         wave(1, 1, 0)
+        second(0, [2], "u2")
         wave(1, 1, 1)
         weave_z(1, 1)
         place(0, 0)

@@ -22,6 +22,7 @@ PACK = 4
 PASS = P * PACK
 CH = 512
 LC = CH // 16
+SPLIT_STEPS = (0, 1, 2, 3)
 ROUND = 1.5 * 2.0**23
 
 
@@ -138,6 +139,7 @@ def tile_list_moire_risk_meter_kernel(tc, tab_words, tab_scales, tab2_words, tab
 
         w1q = {}
         w2q = {}
+        w2grouped = {}
         zq = {}
 
         def prep_w1(a, b):
@@ -150,7 +152,7 @@ def tile_list_moire_risk_meter_kernel(tc, tab_words, tab_scales, tab2_words, tab
             grouped = work.tile([P, PACK * CH], BF16, name="wbf", tag="wbf", align_bytes=64)
             nc.scalar.copy(grouped[:].rearrange("p (m e i) -> p m i e", e=4, i=PACK),
                            raw[:].rearrange("p i (m e) -> p m i e", e=4))
-            w2q[b] = quantize("w2q%d" % b, grouped)
+            w2grouped[b] = grouped
 
         phase = {}
         zrows = {}
@@ -158,7 +160,7 @@ def tile_list_moire_risk_meter_kernel(tc, tab_words, tab_scales, tab2_words, tab
         def products(c, b, h):
             cols = slice(c * CH, (c + 1) * CH)
             u = kt("u", [P, 2, CH], F32, "u%d" % (2 * b + h))
-            lens = kt("lens", [P, 2, CH], F32, "lens%d" % h)
+            lens = kt("lens", [P, 2, CH], F32, "lens%d" % ((4 * c + 2 * b + h) % 3))
             for s in range(2):
                 t = 2 * h + s
                 p1 = psum.tile([P, CH], F32, name="p1", tag="p1")
@@ -178,28 +180,40 @@ def tile_list_moire_risk_meter_kernel(tc, tab_words, tab_scales, tab2_words, tab
                 nc.vector.tensor_tensor(lens[:, s, :], p2[:], d, ALU.add)
             nc.vector.scalar_tensor_tensor(u[:], lens[:], 1.0 / (2.0 * math.pi), u[:], ALU.mult, ALU.max)
             turns = kt("turns", [P, 2, CH], I32, "turns%d" % h)
+            whole = None
             if (c, b, h) == (1, 1, 1):
                 nc.scalar.activation(turns[:].bitcast(U32), u[:], ACT.Copy, bias=ROUND)
-            else:
+            elif 4 * c + 2 * b + h not in SPLIT_STEPS:
                 nc.gpsimd.tensor_scalar(turns[:], u[:], 1.0, ROUND, ALU.mult, ALU.add)
-            phase[c, b, h] = (u, turns)
+            else:
+                nc.gpsimd.tensor_scalar(turns[:, 0, :], u[:, 0, :], 1.0, ROUND, ALU.mult, ALU.add)
+                nc.scalar.activation(turns[:, 1, :].bitcast(U32), u[:, 1, :], ACT.Copy, bias=ROUND)
+                whole = kt("whole", [P, CH], F32, "whole%d" % h)
+                nc.scalar.activation(whole[:], turns[:, 1, :].bitcast(U32), ACT.Copy, bias=-ROUND)
+            phase[c, b, h] = (u, turns, whole)
 
         rests = {}
 
         def reduce_phase(c, b, h):
-            u, turns = phase[c, b, h]
-            rest = u
-            nc.vector.scalar_tensor_tensor(rest[:], turns[:], ROUND, u[:], ALU.subtract, ALU.subtract)
-            rests[c, b, h] = rest
+            u, turns, whole = phase[c, b, h]
+            if whole is None:
+                nc.vector.scalar_tensor_tensor(u[:], turns[:], ROUND, u[:], ALU.subtract, ALU.subtract)
+                rests[c, b, h] = [u[:, 0, :], u[:, 1, :]]
+            else:
+                nc.vector.scalar_tensor_tensor(u[:, 0, :], turns[:, 0, :], ROUND, u[:, 0, :], ALU.subtract, ALU.subtract)
+                rest = kt("rest", [P, CH], F32, "lens%d" % ((4 * c + 2 * b + h + 1) % 3))
+                nc.gpsimd.tensor_tensor(rest[:], whole[:], u[:, 1, :], ALU.subtract)
+                rests[c, b, h] = [u[:, 0, :], rest[:]]
 
         def wave(c, b, h):
             rest = rests[c, b, h]
-            nc.scalar.activation(rest[:], rest[:], ACT.Sin, scale=-2.0 * math.pi)
+            for s in range(2):
+                nc.scalar.activation(rest[s], rest[s], ACT.Sin, scale=-2.0 * math.pi)
             if h == 0:
                 zrows[c, b] = kt("zrows", [P, PACK, CH], BF16, "zrows%d" % b)
             for s in range(2):
                 t = 2 * h + s
-                nc.scalar.activation(zrows[c, b][:, t, :], rest[:, s, :], ACT.Copy, scale=gains[:, b, t:t + 1])
+                nc.scalar.activation(zrows[c, b][:, t, :], rest[s], ACT.Copy, scale=gains[:, b, t:t + 1])
 
         zgrouped = {}
 
@@ -273,9 +287,11 @@ def tile_list_moire_risk_meter_kernel(tc, tab_words, tab_scales, tab2_words, tab
         products(1, 0, 0)
         beats(0, 1, 1)
         weave_z(0, 1)
+        w2q[0] = quantize("w2q0", w2grouped[0])
         quantize_z(0, 0)
         products(1, 0, 1)
         beats(1, 0, 0)
+        w2q[1] = quantize("w2q1", w2grouped[1])
         products(1, 1, 0)
         quantize_z(0, 1)
         beats(1, 0, 1)

import math
from contextlib import ExitStack

import concourse.mybir as mybir

K, M, H, N, T, S, T2 = 1024, 512, 1024, 512, 2048, 1024, 2048
FLOPS = 2 * (K * H * S + M * H * S + H * N * S)

F32 = mybir.dt.float32
BF16 = mybir.dt.bfloat16
I32 = mybir.dt.int32
U32 = mybir.dt.uint32
U16 = mybir.dt.uint16
U8 = mybir.dt.uint8
FP8X4 = mybir.dt.float8_e4m3fn_x4
FP4X4 = mybir.dt.float4_e2m1fn_x4
ALU = mybir.AluOpType
ACT = mybir.ActivationFunctionType

P = 128
PACK = 4
PASS = P * PACK
CH = 512
LC = CH // 16
SPLIT_STEPS = (0, 1, 2, 3)
ROUND = 1.5 * 2.0**23


def tile_list_moire_risk_meter_kernel(tc, tab_words, tab_scales, tab2_words, tab2_scales, offs, offs2, offs3,
                                                w1, w4_words, w4_scales, dist, gain, w2, page1, wgo, out):
    nc = tc.nc
    with ExitStack() as ctx:
        keep = ctx.enter_context(tc.tile_pool(name="keep", bufs=1))
        work = ctx.enter_context(tc.tile_pool(name="work", bufs=2))
        psum = ctx.enter_context(tc.psum_pool(name="psum", bufs=3))

        def kt(name, shape, dtype, slot=None):
            return keep.tile(shape, dtype, name=name, tag=slot or name, align_bytes=64)

        list1 = kt("list1", [P, S // 16], U16)
        list2 = kt("list2", [P, S // 16], U16)
        list3 = kt("list3", [P, S // 16], U16)
        ts_win = kt("ts_win", [P, T], U8, "slot_s")
        t2s_win = kt("t2s_win", [P, T], U8, "slot_t")
        nc.gpsimd.memset(ts_win[:].bitcast(I32), 0)
        nc.vector.memset(t2s_win[:].bitcast(I32), 0)
        w4_raw = kt("w4_raw", [P, 2 * H], U8, "slot_w4")
        gains = kt("gains", [P, 2, PACK], F32)

        def load_words(name, src):
            words = kt(name, [P, T], I32)
            nc.sync.dma_start(words[:], src.rearrange("p t i -> p (t i)").bitcast(I32))
            return words

        def load_rows(slot, src):
            raw = kt("raw", [P, PACK, CH], F32, slot)
            nc.sync.dma_start(raw[:], src.rearrange("(p i) c -> p i c", i=PACK))
            return raw

        def load_w1(a, b):
            return load_rows("slot_w%d" % a, w1[a * PASS:(a + 1) * PASS, b * PASS:(b + 1) * PASS])

        dist_sb = {}

        def load_dist(c, b, halves=range(2)):
            rows = dist[b * PASS:(b + 1) * PASS, c * CH:(c + 1) * CH].rearrange("(p t) j -> p t j", t=PACK)
            for h in halves:
                dist_sb[c, b, h] = kt("dist", [P, 2, CH], F32, "dist%d%d" % (b, h))
                nc.sync.dma_start(dist_sb[c, b, h][:], rows[:, 2 * h:2 * h + 2, :])

        def load_page(n, slot):
            page = kt("page", [P, T2], F32, slot)
            nc.sync.dma_start(page[:], page1[n * P:(n + 1) * P, :])
            return page

        w4s_raw = kt("w4s_raw", [P, H], U8)
        nc.gpsimd.memset(w4s_raw[:].bitcast(I32), 0)

        def load_plane(plane, rows, q):
            nc.sync.dma_start(plane[32 * q:32 * q + 4, :].bitcast(I32), rows[0, 4 * q:4 * q + 4, :].bitcast(I32))

        nc.sync.dma_start(list1[:], offs)
        tabw = [load_words("tabw0", tab_words[0])]
        nc.sync.dma_start(list2[:], offs2)
        nc.sync.dma_start(w4_raw[:].bitcast(I32), w4_words[0].bitcast(I32))
        for a in range(2):
            for e in range(2):
                nc.sync.dma_start(ts_win[4 * a + e:P:16, :].bitcast(I32), tab_scales[a, e:16:2, :].bitcast(I32))
        w1raw = {(0, 0): load_w1(0, 0)}
        tabw.append(load_words("tabw1", tab_words[1]))
        for q in range(4):
            load_plane(t2s_win, tab2_scales, q)
        for q in range(2):
            load_plane(w4s_raw, w4_scales, q)
        w1raw[1, 0] = load_w1(1, 0)

        ts_g = kt("ts_g", [P, S], U8)
        v_scales = kt("v_scales", [P, S], U8)
        nc.vector.tensor_copy(ts_g[:], ts_win[:].indirect(list1[:]))
        nc.vector.tensor_copy(v_scales[:].bitcast(I32), ts_g[:].bitcast(I32))
        v2_scales = kt("v2_scales", [P, S], U8)
        nc.vector.tensor_copy(v2_scales[:], t2s_win[:].indirect(list2[:]))

        v_words = {}
        v2_words = {}

        def gather_tab(a, c):
            v_words[a, c] = kt("vw%d%d" % (a, c), [P, CH], U32)
            nc.vector.tensor_copy(v_words[a, c][:], tabw[a][:].bitcast(U32).indirect(list1[:, c * LC:(c + 1) * LC]))

        def gather_tab2(c):
            v2_words[c] = kt("v2w%d" % c, [P, CH], U32)
            nc.vector.tensor_copy(v2_words[c][:], tab2w[:].bitcast(U32).indirect(list2[:, c * LC:(c + 1) * LC]))

        gather_tab(0, 0)
        gather_tab(0, 1)
        tab2w = load_words("tab2w", tab2_words[0])
        for a in range(2):
            for e in range(2):
                nc.sync.dma_start(v_scales[4 * a + 2 + e:P:32, :].bitcast(I32), ts_g[16 + 4 * a + e:P:32, :].bitcast(I32))
        for q in range(2, 4):
            load_plane(w4s_raw, w4_scales, q)

        w4_p = kt("w4_p", [P, 2, 2 * PASS], U8)
        w4s_p = kt("w4s_p", [P, 2, PASS], U8)
        for b in range(2):
            nc.vector.tensor_copy(
                w4_p[:, b, :].bitcast(U16).rearrange("p (t q) -> p t q", t=PACK),
                w4_raw[:, 2 * PASS * b:2 * PASS * (b + 1)].bitcast(U16).rearrange("p (q t) -> p t q", t=PACK))
            nc.vector.tensor_copy(
                w4s_p[:, b, :].rearrange("p (t q) -> p t q", t=PACK),
                w4s_raw[:, PASS * b:PASS * (b + 1)].rearrange("p (q t) -> p t q", t=PACK))

        def quantize(name, grouped):
            codes = kt(name + "c", [P, CH], U32)
            scales = kt(name + "s", [P, CH], U8)
            nc.vector.quantize_mx(out=codes[:].bitcast(FP8X4), scales=scales[:], in_=grouped[:])
            return codes, scales

        w1q = {}
        w2q = {}
        w2grouped = {}
        zq = {}

        def prep_w1(a, b):
            grouped = work.tile([P, PACK * CH], BF16, name="wbf", tag="wbf", align_bytes=64)
            nc.scalar.copy(grouped[:].rearrange("p (t m i) -> p m i t", t=PACK, i=PACK),
                           w1raw[a, b][:].rearrange("p i (m t) -> p m i t", t=PACK))
            w1q[a, b] = quantize("w1q%d%d" % (a, b), grouped)

        def prep_w2(b, raw):
            grouped = work.tile([P, PACK * CH], BF16, name="wbf", tag="wbf", align_bytes=64)
            nc.scalar.copy(grouped[:].rearrange("p (m e i) -> p m i e", e=4, i=PACK),
                           raw[:].rearrange("p i (m e) -> p m i e", e=4))
            w2grouped[b] = grouped

        phase = {}
        zrows = {}

        def products(c, b, h):
            cols = slice(c * CH, (c + 1) * CH)
            u = kt("u", [P, 2, CH], F32, "u%d" % (2 * b + h))
            lens = kt("lens", [P, 2, CH], F32, "lens%d" % ((4 * c + 2 * b + h) % 3))
            for s in range(2):
                t = 2 * h + s
                p1 = psum.tile([P, CH], F32, name="p1", tag="p1")
                p2 = psum.tile([P, CH], F32, name="p2", tag="p2")
                for a in range(2):
                    codes, scales = w1q[a, b]
                    nc.tensor.matmul_mx(out=p1[:], lhsT=codes[:, t * P:(t + 1) * P].bitcast(FP8X4),
                                        lhsT_scale=scales[:, t * P:(t + 1) * P],
                                        rhs=v_words[a, c][:].bitcast(FP8X4), rhs_scale=v_scales[4 * a:P, cols],
                                        start=(a == 0), stop=(a == 1))
                nc.tensor.matmul_mx(out=p2[:], lhsT=w4_p[:, b, 2 * P * t:2 * P * (t + 1)].bitcast(FP4X4),
                                    lhsT_scale=w4s_p[:, b, t * P:(t + 1) * P],
                                    rhs=v2_words[c][:].bitcast(FP8X4), rhs_scale=v2_scales[:, cols],
                                    start=True, stop=True)
                d = dist_sb[c, b, h][:, s, :]
                nc.vector.scalar_tensor_tensor(u[:, s, :], p1[:], 1.0 / (2.0 * math.pi), d, ALU.mult, ALU.mult)
                nc.vector.tensor_tensor(lens[:, s, :], p2[:], d, ALU.add)
            nc.vector.scalar_tensor_tensor(u[:], lens[:], 1.0 / (2.0 * math.pi), u[:], ALU.mult, ALU.max)
            turns = kt("turns", [P, 2, CH], I32, "turns%d" % h)
            whole = None
            if (c, b, h) == (1, 1, 1):
                nc.scalar.activation(turns[:].bitcast(U32), u[:], ACT.Copy, bias=ROUND)
            elif 4 * c + 2 * b + h not in SPLIT_STEPS:
                nc.gpsimd.tensor_scalar(turns[:], u[:], 1.0, ROUND, ALU.mult, ALU.add)
            else:
                nc.gpsimd.tensor_scalar(turns[:, 0, :], u[:, 0, :], 1.0, ROUND, ALU.mult, ALU.add)
                nc.scalar.activation(turns[:, 1, :].bitcast(U32), u[:, 1, :], ACT.Copy, bias=ROUND)
                whole = kt("whole", [P, CH], F32, "whole%d" % h)
                nc.scalar.activation(whole[:], turns[:, 1, :].bitcast(U32), ACT.Copy, bias=-ROUND)
            phase[c, b, h] = (u, turns, whole)

        rests = {}

        def reduce_phase(c, b, h):
            u, turns, whole = phase[c, b, h]
            if whole is None:
                nc.vector.scalar_tensor_tensor(u[:], turns[:], ROUND, u[:], ALU.subtract, ALU.subtract)
                rests[c, b, h] = [u[:, 0, :], u[:, 1, :]]
            else:
                nc.vector.scalar_tensor_tensor(u[:, 0, :], turns[:, 0, :], ROUND, u[:, 0, :], ALU.subtract, ALU.subtract)
                rest = kt("rest", [P, CH], F32, "lens%d" % ((4 * c + 2 * b + h + 1) % 3))
                nc.gpsimd.tensor_tensor(rest[:], whole[:], u[:, 1, :], ALU.subtract)
                rests[c, b, h] = [u[:, 0, :], rest[:]]

        def wave(c, b, h):
            rest = rests[c, b, h]
            for s in range(2):
                nc.scalar.activation(rest[s], rest[s], ACT.Sin, scale=-2.0 * math.pi)
            if h == 0:
                zrows[c, b] = kt("zrows", [P, PACK, CH], BF16, "zrows%d" % b)
            for s in range(2):
                t = 2 * h + s
                nc.scalar.activation(zrows[c, b][:, t, :], rest[s], ACT.Copy, scale=gains[:, b, t:t + 1])

        zgrouped = {}

        def beats(c, b, h):
            reduce_phase(c, b, h)
            wave(c, b, h)

        def weave_z(c, b):
            grouped = work.tile([P, PACK * CH], BF16, name="zbf", tag="zbf", align_bytes=64)
            nc.scalar.copy(grouped[:].rearrange("p (m e t) -> p m t e", e=4, t=PACK),
                           zrows[c, b][:].rearrange("p t (m e) -> p m t e", e=4))
            zgrouped[c, b] = grouped

        def quantize_z(c, b):
            grouped = zgrouped[c, b]
            codes = work.tile([P, CH], U32, name="zc", tag="zc", bufs=4, align_bytes=64)
            scales = work.tile([P, CH], U8, name="zs", tag="zs", bufs=4, align_bytes=64)
            nc.vector.quantize_mx(out=codes[:].bitcast(FP8X4), scales=scales[:], in_=grouped[:])
            zq[c, b] = (codes, scales)

        scores = {}

        def second(c, tiles, tag=None):
            for n in tiles:
                y = psum.tile([P, CH], F32, name="y", tag="y", bufs=2)
                for b in range(2):
                    nc.tensor.matmul_mx(out=y[:], lhsT=w2q[b][0][:, n * P:(n + 1) * P].bitcast(FP8X4),
                                        lhsT_scale=w2q[b][1][:, n * P:(n + 1) * P],
                                        rhs=zq[c, b][0][:].bitcast(FP8X4), rhs_scale=zq[c, b][1][:],
                                        start=(b == 0), stop=(b == 1))
                scores[c, n] = kt("score", [P, CH], F32, tag or "score%d" % n)
                nc.scalar.copy(scores[c, n][:], y[:])

        def place(c, n):
            nc.vector.tensor_tensor(pages[n][:].indirect(list3[:, c * LC:(c + 1) * LC]), scores[c, n][:],
                                    wgo_sb[:, c * CH:(c + 1) * CH], ALU.mult)

        prep_w1(0, 0)
        gather_tab(1, 0)
        prep_w1(1, 0)
        gather_tab2(0)
        load_dist(0, 0, [0])
        w1raw[0, 1] = load_w1(0, 1)
        load_dist(0, 0, [1])
        w1raw[1, 1] = load_w1(1, 1)
        prep_w1(0, 1)
        gather_tab(1, 1)
        prep_w1(1, 1)
        load_dist(0, 1)
        nc.sync.dma_start(gains[:], gain.rearrange("(b p t) -> p b t", b=2, t=PACK))
        w2raw = [load_rows("tabw%d" % b, w2[b * PASS:(b + 1) * PASS, :]) for b in range(2)]
        nc.sync.dma_start(list3[:], offs3)
        products(0, 0, 0)
        gather_tab2(1)
        products(0, 0, 1)
        load_dist(1, 0)
        beats(0, 0, 0)
        products(0, 1, 0)
        beats(0, 0, 1)
        weave_z(0, 0)
        prep_w2(0, w2raw[0])
        products(0, 1, 1)
        load_dist(1, 1)
        wgo_sb = kt("wgo_sb", [P, S], F32, "slot_w0")
        nc.sync.dma_start(wgo_sb[:], wgo)
        beats(0, 1, 0)
        prep_w2(1, w2raw[1])
        pages = [load_page(b, "tabw%d" % b) for b in range(2)]
        pages.append(load_page(2, "tab2w"))
        pages.append(load_page(3, "slot_w1"))
        products(1, 0, 0)
        beats(0, 1, 1)
        weave_z(0, 1)
        w2q[0] = quantize("w2q0", w2grouped[0])
        quantize_z(0, 0)
        products(1, 0, 1)
        beats(1, 0, 0)
        w2q[1] = quantize("w2q1", w2grouped[1])
        products(1, 1, 0)
        quantize_z(0, 1)
        beats(1, 0, 1)
        second(0, [0], "u1")
        weave_z(1, 0)
        products(1, 1, 1)
        reduce_phase(1, 1, 0)
        reduce_phase(1, 1, 1)
        second(0, [1], "turns1")
        wave(1, 1, 0)
        second(0, [2], "u2")
        wave(1, 1, 1)
        weave_z(1, 1)
        place(0, 0)
        place(0, 1)
        quantize_z(1, 0)
        place(0, 2)
        quantize_z(1, 1)
        second(0, [3], "zrows1")
        place(0, 3)
        second(1, range(N // P))
        for n in range(N // P):
            place(1, n)
            nc.sync.dma_start(out[n * P:(n + 1) * P, :], pages[n][:])
